import numpy as np
CORES = [388,396,404,412,420,428,436,444,452,460,468,476,484,492,500,508,124,252,380]
N = 19
ROOT = 7
def setup_inputs(rng):
    return {"x": rng.standard_normal((N, 128, 256), dtype=np.float32)}
def reference(x):
    return {"y": np.broadcast_to(x[ROOT], x.shape)}

@@ -1,0 +1,56 @@
+from concourse.bass import DstId, RemoteDMATransfer
+
+SCRATCH = {
+    "buf": ("sbuf", [128, 256], "float32"),
+}
+SEMAPHORES = ["loaded", "arrived", "sent", "stored"]
+
+OFF = 0x00FF
+NE = 8
+
+
+def _plan(T):
+    root = T.cores[T.root]
+    h3 = (root // 128) * 128
+    plan = {root: [h3 + 8 * j + 6 for j in range(1, 16, 2)] + [2 * 128 + 15 * 8 + 4]}
+    for j in range(1, 16, 2):
+        relay = h3 + 8 * j + 6
+        d = [h3 + 8 * (j - 1) + 4]
+        if h3 + 8 * j + 4 != root:
+            d.append(h3 + 8 * j + 4)
+        if j == 15:
+            d.append(0 * 128 + 15 * 8 + 4)
+        plan[relay] = d
+    plan[2 * 128 + 15 * 8 + 4] = [1 * 128 + 15 * 8 + 4]
+    return root, plan
+
+
+def rank_program(g, core, T, topo):
+    root, plan = _plan(T)
+    dests = plan.get(core, [])
+    rank = T.rank_of(core)
+    if rank is None and not dests:
+        return
+
+    if core == root:
+        g.sync.dma_start(T.buf[:], T.x[:]).then_inc(T.sem.loaded, 16)
+        g.scalar.dma_start(T.y[:], T.x[:]).then_inc(T.sem.stored, 16)
+        g.wait_ge(T.sem.loaded, 16)
+    else:
+        g.wait_ge(T.sem.arrived, NE)
+        if rank is not None:
+            g.sync.wait_ge(T.sem.arrived, NE)
+            g.sync.dma_start(T.y[:], T.buf[:]).then_inc(T.sem.stored, 16)
+
+    if dests:
+        ids = []
+        for d in dests:
+            rid, pid = topo.addr(d, core)
+            ids.append(DstId(rid=rid, pnc=pid))
+        g.remote_dma_fused(
+            [RemoteDMATransfer(dst_ids=ids, dma_engine_mask=OFF, remote_sem=T.sem.arrived,
+                               srcs=[T.buf[:]], dsts=[T.buf[:] for _ in dests])],
+            local_sem=T.sem.sent)
+        g.wait_ge(T.sem.sent, NE)
+    if rank is not None:
+        g.wait_ge(T.sem.stored, 16)

@@ -1,56 +1,65 @@
 from concourse.bass import DstId, RemoteDMATransfer
 
+NP = 16
 SCRATCH = {
-    "buf": ("sbuf", [128, 256], "float32"),
+    "buf": ("dram", [NP, 128, 16], "float32"),
 }
 SEMAPHORES = ["loaded", "arrived", "sent", "stored"]
 
-OFF = 0x00FF
-NE = 8
+
+def _core(h, chip, c):
+    return h * 128 + chip * 8 + c
 
 
 def _plan(T):
     root = T.cores[T.root]
-    h3 = (root // 128) * 128
-    plan = {root: [h3 + 8 * j + 6 for j in range(1, 16, 2)] + [2 * 128 + 15 * 8 + 4]}
-    for j in range(1, 16, 2):
-        relay = h3 + 8 * j + 6
-        d = [h3 + 8 * (j - 1) + 4]
-        if h3 + 8 * j + 4 != root:
-            d.append(h3 + 8 * j + 4)
-        if j == 15:
-            d.append(0 * 128 + 15 * 8 + 4)
-        plan[relay] = d
-    plan[2 * 128 + 15 * 8 + 4] = [1 * 128 + 15 * 8 + 4]
-    return root, plan
+    chips = [(3, j) for j in (1, 3, 5, 9, 11, 13, 15)] + [(2, j) for j in range(1, 16, 2)]
+    holders = [_core(h, j, 6 if i % 2 == 0 else 2) for i, (h, j) in enumerate(chips)]
+    holders.append(_core(2, 15, 2))
+    helpers = [_core(0, 7, k) for k in range(8)]
+    near = [c for c in T.cores if c // 128 >= 2 and c != root]
+    far = [c for c in T.cores if c // 128 < 2]
+    return root, holders, helpers, near, far
+
+
+def _transfer(T, topo, core, piece, dests, mask):
+    ids = []
+    for d in dests:
+        rid, pid = topo.addr(d, core)
+        ids.append(DstId(rid=rid, pnc=pid))
+    return RemoteDMATransfer(dst_ids=ids, dma_engine_mask=mask, remote_sem=T.sem.arrived,
+                             srcs=[T.buf[piece]], dsts=[T.buf[piece] for _ in dests])
 
 
 def rank_program(g, core, T, topo):
-    root, plan = _plan(T)
-    dests = plan.get(core, [])
-    rank = T.rank_of(core)
-    if rank is None and not dests:
-        return
+    root, holders, helpers, near, far = _plan(T)
 
     if core == root:
         g.sync.dma_start(T.buf[:], T.x[:]).then_inc(T.sem.loaded, 16)
         g.scalar.dma_start(T.y[:], T.x[:]).then_inc(T.sem.stored, 16)
         g.wait_ge(T.sem.loaded, 16)
-    else:
-        g.wait_ge(T.sem.arrived, NE)
-        if rank is not None:
-            g.sync.wait_ge(T.sem.arrived, NE)
-            g.sync.dma_start(T.y[:], T.buf[:]).then_inc(T.sem.stored, 16)
-
-    if dests:
-        ids = []
-        for d in dests:
-            rid, pid = topo.addr(d, core)
-            ids.append(DstId(rid=rid, pnc=pid))
+        for half in range(2):
+            g.remote_dma_fused(
+                [_transfer(T, topo, core, 8 * half + e, [holders[8 * half + e], helpers[e]], 1 << e)
+                 for e in range(8)],
+                local_sem=T.sem.sent)
+        g.wait_ge(T.sem.sent, 16)
+        g.wait_ge(T.sem.stored, 16)
+    elif core in holders:
+        k = holders.index(core)
+        g.wait_ge(T.sem.arrived, 1)
         g.remote_dma_fused(
-            [RemoteDMATransfer(dst_ids=ids, dma_engine_mask=OFF, remote_sem=T.sem.arrived,
-                               srcs=[T.buf[:]], dsts=[T.buf[:] for _ in dests])],
+            [_transfer(T, topo, core, k, near[2 * e:2 * e + 2], 1 << e) for e in range(8)],
             local_sem=T.sem.sent)
-        g.wait_ge(T.sem.sent, NE)
-    if rank is not None:
+        g.wait_ge(T.sem.sent, 8)
+    elif core in helpers:
+        k = helpers.index(core)
+        g.wait_ge(T.sem.arrived, 2)
+        g.remote_dma_fused(
+            [_transfer(T, topo, core, k + 8 * (i // 2), [far[i % 2]], 3 << (2 * i)) for i in range(4)],
+            local_sem=T.sem.sent)
+        g.wait_ge(T.sem.sent, 8)
+    elif core in near or core in far:
+        g.wait_ge(T.sem.arrived, NP * (1 if core in near else 2))
+        g.dma_start(T.y[:], T.buf[:]).then_inc(T.sem.stored, 16)
         g.wait_ge(T.sem.stored, 16)

from concourse.bass import DstId, RemoteDMATransfer

NP = 16
SCRATCH = {
    "buf": ("dram", [NP, 128, 16], "float32"),
}
SEMAPHORES = ["loaded", "arrived", "sent", "stored"]


def _core(h, chip, c):
    return h * 128 + chip * 8 + c


def _plan(T):
    root = T.cores[T.root]
    chips = [(3, j) for j in (1, 3, 5, 9, 11, 13, 15)] + [(2, j) for j in range(1, 16, 2)]
    holders = [_core(h, j, 6 if i % 2 == 0 else 2) for i, (h, j) in enumerate(chips)]
    holders.append(_core(2, 15, 2))
    helpers = [_core(0, 7, k) for k in range(8)]
    near = [c for c in T.cores if c // 128 >= 2 and c != root]
    far = [c for c in T.cores if c // 128 < 2]
    return root, holders, helpers, near, far


def _transfer(T, topo, core, piece, dests, mask):
    ids = []
    for d in dests:
        rid, pid = topo.addr(d, core)
        ids.append(DstId(rid=rid, pnc=pid))
    return RemoteDMATransfer(dst_ids=ids, dma_engine_mask=mask, remote_sem=T.sem.arrived,
                             srcs=[T.buf[piece]], dsts=[T.buf[piece] for _ in dests])


def rank_program(g, core, T, topo):
    root, holders, helpers, near, far = _plan(T)

    if core == root:
        g.sync.dma_start(T.buf[:], T.x[:]).then_inc(T.sem.loaded, 16)
        g.scalar.dma_start(T.y[:], T.x[:]).then_inc(T.sem.stored, 16)
        g.wait_ge(T.sem.loaded, 16)
        for half in range(2):
            g.remote_dma_fused(
                [_transfer(T, topo, core, 8 * half + e, [holders[8 * half + e], helpers[e]], 1 << e)
                 for e in range(8)],
                local_sem=T.sem.sent)
        g.wait_ge(T.sem.sent, 16)
        g.wait_ge(T.sem.stored, 16)
    elif core in holders:
        k = holders.index(core)
        g.wait_ge(T.sem.arrived, 1)
        g.remote_dma_fused(
            [_transfer(T, topo, core, k, near[2 * e:2 * e + 2], 1 << e) for e in range(8)],
            local_sem=T.sem.sent)
        g.wait_ge(T.sem.sent, 8)
    elif core in helpers:
        k = helpers.index(core)
        g.wait_ge(T.sem.arrived, 2)
        g.remote_dma_fused(
            [_transfer(T, topo, core, k + 8 * (i // 2), [far[i % 2]], 3 << (2 * i)) for i in range(4)],
            local_sem=T.sem.sent)
        g.wait_ge(T.sem.sent, 8)
    elif core in near or core in far:
        g.wait_ge(T.sem.arrived, NP * (1 if core in near else 2))
        g.dma_start(T.y[:], T.buf[:]).then_inc(T.sem.stored, 16)
        g.wait_ge(T.sem.stored, 16)
